import numpy as np
import ml_dtypes


def mxq(x, axis, fmt="e4m3"):
    dtype, down = {"e4m3": (ml_dtypes.float8_e4m3fn, 7), "e5m2": (ml_dtypes.float8_e5m2, 14)}[fmt]
    v = np.moveaxis(np.asarray(x, np.float32).astype(ml_dtypes.bfloat16).astype(np.float64), axis, -1)
    blocks = v.reshape(v.shape[:-1] + (-1, 32))
    amax = np.abs(blocks).max(-1, keepdims=True)
    byte = np.maximum(np.where(amax > 0, np.frexp(amax)[1] - 1 + 127, 0) - down, 1)
    scale = np.exp2(byte - 127.0)
    codes = (blocks / scale).astype(np.float32).astype(dtype).astype(np.float64)
    return np.moveaxis((codes * scale).reshape(v.shape), -1, axis)


WIDE = False


def mx_kscale(k):
    if not WIDE:
        return np.ones(k)
    levels = np.array([10, -10, 5, -5, 0])
    if k % 512:
        return np.exp2(np.random.permutation(np.resize(levels, k // 32))).repeat(32)
    a = np.empty((k // 512, 16))
    for p in range(k // 512):
        a[p, :8] = np.random.permutation(np.resize(levels, 8))
        for g in range(8):
            far = levels[np.abs(levels - a[p, g]) >= 10]
            a[p, g + 8] = far[np.random.randint(len(far))]
    return np.exp2(a.ravel()).repeat(32)


def f64(x):
    return np.asarray(x).astype(np.float64)


def striped(idx):
    return np.tile(idx.reshape(-1, 16).T, (8, 1)).astype(np.uint16)


def unstriped(offs):
    return offs[:16].T.reshape(-1).astype(np.int64)


def striped8(idx):
    return np.concatenate([x.reshape(-1, 16).T for x in idx]).astype(np.uint16)


def runs(offs, k):
    lists = np.stack([offs[16 * r : 16 * r + 16].T.reshape(-1) for r in range(8)]).astype(np.int64)
    return lists[np.arange(k) % 512 // 64]


def pack_weight(w):
    k, n = w.shape
    w = f64(np.asarray(w, np.float32).astype(ml_dtypes.bfloat16)).reshape(k // 32, 32, n)
    amax = np.abs(w).max(1)
    byte = np.clip(np.where(amax > 0, np.frexp(amax)[1] - 1 + 127 - 7, 1), 1, 254)
    scaled = (w * np.exp2(127.0 - byte)[:, None, :]).reshape(k, n).astype(np.float32)
    words = np.ascontiguousarray(scaled.reshape(k // 512, 128, 4, n).transpose(0, 1, 3, 2)).astype(ml_dtypes.float8_e4m3fn).view(np.uint8)
    return words, np.ascontiguousarray(byte.astype(np.uint8).reshape(k // 512, 16, n))


def unpack_weight(words, scales):
    g, p, n, _ = words.shape
    vals = np.ascontiguousarray(words).view(ml_dtypes.float8_e4m3fn).astype(np.float64) * np.repeat(np.exp2(scales.astype(np.float64) - 127.0), 8, axis=1)[..., None]
    return vals.transpose(0, 1, 3, 2).reshape(g * 512, n)


K, T, S, G, H, W = 512, 1024, 256, 2048, 512, 128


def setup_inputs():
    n = np.random.standard_normal
    s = mx_kscale(K)[:, None]
    packed_xT = pack_weight(n((K, T)) * s)
    packed_dT = pack_weight(n((K, G)) / s)
    perm = np.random.permutation(S)
    return {
        "x_words": packed_xT[0],
        "x_scales": packed_xT[1],
        "d_words": packed_dT[0],
        "d_scales": packed_dT[1],
        "gs": (np.random.uniform(0.5, 1.5, (K, 1)) * s).astype(np.float32),
        "offs": striped8(np.random.randint(0, T, (8, S))),
        "k1": striped8(np.random.randint(0, G, (8, H))),
        "n1": striped(np.random.permutation(S)),
        "k2": striped8(np.random.randint(0, G, (8, H))),
        "n2": striped(perm[:W]),
        "n3": striped(perm[W:]),
    }


def reference(x_words, x_scales, d_words, d_scales, gs, offs, k1, n1, k2, n2, n3):
    d_k2 = unpack_weight(d_words, d_scales)[np.arange(K)[:, None], runs(k2, K)]
    d_k1 = unpack_weight(d_words, d_scales)[np.arange(K)[:, None], runs(k1, K)]
    xq = unpack_weight(x_words, x_scales)[np.arange(K)[:, None], runs(offs, K)]
    h = 0.0625 * (d_k1.T @ xq)
    ds = np.zeros((H, S))
    ds[:, unstriped(n1)] = h
    z = f64(gs) * (h - ds)
    h2 = 0.0625 * ((d_k2.T @ mxq(z, 0, "e4m3")))
    pb = h2[:, unstriped(n3)]
    pa = h2[:, unstriped(n2)]
    rb = pb - (0.5 * pa)
    ra = np.sqrt((pa) ** 2 + (pb) ** 2 + 0.25)
    ds2 = np.zeros((H, S))
    ds2[:, unstriped(n2)] = ra
    out = ds2.copy()
    out[:, unstriped(n3)] = rb
    return out

@@ -1,0 +1,137 @@
+from contextlib import ExitStack
+
+import concourse.mybir as mybir
+
+F32 = mybir.dt.float32
+BF16 = mybir.dt.bfloat16
+I32 = mybir.dt.int32
+U32 = mybir.dt.uint32
+U16 = mybir.dt.uint16
+U8 = mybir.dt.uint8
+FP8X4 = mybir.dt.float8_e4m3fn_x4
+ALU = mybir.AluOpType
+ACT = mybir.ActivationFunctionType
+
+P = 128
+PACK = 4
+T, S, G, H, W = 1024, 256, 2048, 512, 128
+HALF = S // 2
+FLOPS = 2 * 2 * 512 * H * S
+
+
+def first_in_halves(tile_number):
+    return [(0, HALF), (HALF, S)] if tile_number == 0 else [(0, S)]
+
+
+def tile_picked_hcodesendmxpolar_none_p_kernel(
+    tc, x_words, x_scales, d_words, d_scales, gs, offs, k1, n1, k2, n2, n3, out
+):
+    nc = tc.nc
+    with ExitStack() as ctx:
+        lists = ctx.enter_context(tc.tile_pool(name="lists", bufs=1))
+        keep = ctx.enter_context(tc.tile_pool(name="keep", bufs=1))
+        psum = ctx.enter_context(tc.psum_pool(name="psum", bufs=8))
+
+        def load_list(name, src):
+            t = lists.tile(list(src.shape), U16, name=name)
+            nc.sync.dma_start(t[:], src)
+            return t
+
+        d_tab = keep.tile([P, G], U32, name="d_tab")
+        x_tab = keep.tile([P, T], U32, name="x_tab")
+        d_stab = keep.tile([P, G], U8, name="d_stab")
+        x_stab = keep.tile([P, T], U8, name="x_stab")
+        plane1 = keep.tile([P, H + S], U8, name="plane1", align_bytes=64)
+        plane2 = keep.tile([P, H], U8, name="plane2", align_bytes=64)
+        gain = keep.tile([P, PACK], F32, name="gain")
+
+        nc.vector.memset(d_stab[:].bitcast(I32), 0)
+        nc.vector.memset(x_stab[:].bitcast(I32), 0)
+        nc.scalar.dma_start(gain[:], gs.rearrange("(p t) o -> p (t o)", t=PACK))
+        k1_l = load_list("k1_l", k1)
+        nc.scalar.dma_start(d_tab[:].bitcast(I32), d_words[0].rearrange("p n t -> p (n t)").bitcast(I32))
+        offs_l = load_list("offs_l", offs)
+        nc.sync.dma_start(d_stab[0:P:8, :].bitcast(I32), d_scales[0].bitcast(I32))
+        nc.sync.dma_start(x_stab[0:P:8, :].bitcast(I32), x_scales[0].bitcast(I32))
+        n1_l = load_list("n1_l", n1)
+        k2_l = load_list("k2_l", k2)
+        nc.sync.dma_start(x_tab[:].bitcast(I32), x_words[0].rearrange("p n t -> p (n t)").bitcast(I32))
+        n2_l = load_list("n2_l", n2)
+        n3_l = load_list("n3_l", n3)
+        nc.vector.memset(plane1[:].bitcast(I32), 0)
+        nc.vector.memset(plane2[:].bitcast(I32), 0)
+
+        def place_rows(plane, picked, queues):
+            for j in range(4):
+                queues[j % len(queues)].dma_start(plane[j:P:32, :].bitcast(I32), picked[8 * j : P : 32, :].bitcast(I32))
+
+        picked1 = keep.tile([P, H + S], U8, name="picked1")
+        nc.vector.tensor_copy(picked1[:, 0:H], d_stab[:].indirect(k1_l[:]))
+        nc.vector.tensor_copy(picked1[:, H : H + S], x_stab[:].indirect(offs_l[:]))
+        place_rows(plane1, picked1, [nc.sync, nc.scalar])
+
+        w1 = keep.tile([P, H], U32, name="w1")
+        nc.vector.tensor_copy(w1[:], d_tab[:].indirect(k1_l[:]))
+        xq = keep.tile([P, S], U32, name="xq", tag="words", align_bytes=64)
+        nc.vector.tensor_copy(xq[:], x_tab[:].indirect(offs_l[:]))
+
+        w1_dealt = keep.tile([P, PACK, P], U32, name="w1_dealt", align_bytes=64)
+        s1_dealt = keep.tile([P, PACK, P], U8, name="s1_dealt", tag="bytes", align_bytes=64)
+        gh, ds = [], []
+        for t in range(PACK):
+            nc.vector.tensor_copy(w1_dealt[:, t, :], w1[:, t:H:PACK])
+            nc.vector.tensor_copy(s1_dealt[:, t, :], plane1[:, t:H:PACK])
+            gh.append(keep.tile([P, S], F32, name=f"gh{t}"))
+            ds.append(keep.tile([P, 2 * S], F32, name=f"ds{t}"))
+            for lo, hi in first_in_halves(t):
+                acc = psum.tile([P, S], F32, name="acc")
+                nc.tensor.matmul_mx(
+                    out=acc[:, lo:hi], lhsT=w1_dealt[:, t, :].bitcast(FP8X4), lhsT_scale=s1_dealt[:, t, :],
+                    rhs=xq[:, lo:hi].bitcast(FP8X4), rhs_scale=plane1[:, H + lo : H + hi], start=True, stop=True,
+                )
+                nc.vector.tensor_scalar(gh[t][:, lo:hi], acc[:, lo:hi], gain[:, t : t + 1], 0.0625, ALU.mult, ALU.mult)
+                nc.scalar.activation(ds[t][:].indirect(n1_l[:, lo // 16 : hi // 16]), gh[t][:, lo:hi], ACT.Copy)
+
+        picked2 = keep.tile([P, H], U8, name="picked2", tag="bytes", align_bytes=64)
+        nc.vector.tensor_copy(picked2[:], d_stab[:].indirect(k2_l[:]))
+        place_rows(plane2, picked2, [nc.sync])
+        w2 = keep.tile([P, H], U32, name="w2", tag="words", align_bytes=64)
+        nc.vector.tensor_copy(w2[:], d_tab[:].indirect(k2_l[:]))
+
+        z = [keep.tile([P, HALF, PACK], BF16, name=f"z{u}", align_bytes=64) for u in range(2)]
+        for t in range(PACK):
+            for u in range(2):
+                cols = slice(u * HALF, (u + 1) * HALF)
+                nc.vector.tensor_tensor(z[u][:, :, t], gh[t][:, cols], ds[t][:, cols], ALU.subtract)
+        zq = keep.tile([P, S], U32, name="zq", align_bytes=64)
+        zs = keep.tile([P, S], U8, name="zs", align_bytes=64)
+        for u in range(2):
+            cols = slice(u * HALF, (u + 1) * HALF)
+            nc.vector.quantize_mx(out=zq[:, cols].bitcast(FP8X4), scales=zs[:, cols], in_=z[u][:].rearrange("p c t -> p (c t)"))
+
+        for m in range(H // P):
+            rows = slice(m * P, (m + 1) * P)
+            h2 = keep.tile([P, S], F32, name=f"h2_{m}")
+            pieces = [slice(0, HALF), slice(HALF, S)] if m == 0 else [slice(0, S)]
+            for cols in pieces:
+                acc = psum.tile([P, S], F32, name="acc")
+                nc.tensor.matmul_mx(
+                    out=acc[:, cols], lhsT=w2[:, rows].bitcast(FP8X4), lhsT_scale=plane2[:, rows],
+                    rhs=zq[:, cols].bitcast(FP8X4), rhs_scale=zs[:, cols], start=True, stop=True,
+                )
+                nc.vector.tensor_scalar(h2[:, cols], acc[:, cols], 0.0625, None, ALU.mult)
+            pab = keep.tile([P, 2, W], F32, name=f"pab{m}")
+            nc.scalar.activation(pab[:, 0, :], h2[:].indirect(n2_l[:]), ACT.Copy)
+            nc.scalar.activation(pab[:, 1, :], h2[:].indirect(n3_l[:]), ACT.Copy)
+            rb = keep.tile([P, W], F32, name=f"rb{m}")
+            nc.vector.scalar_tensor_tensor(rb[:], pab[:, 0, :], -0.5, pab[:, 1, :], ALU.mult, ALU.add)
+            sq = keep.tile([P, 2, W], F32, name=f"sq{m}")
+            nc.vector.tensor_tensor(sq[:], pab[:], pab[:], ALU.mult)
+            radicand = keep.tile([P, W], F32, name=f"radicand{m}")
+            nc.vector.scalar_tensor_tensor(radicand[:], sq[:, 0, :], 0.25, sq[:, 1, :], ALU.add, ALU.add)
+            res = keep.tile([P, S], F32, name=f"res{m}")
+            nc.scalar.activation(res[:].indirect(n3_l[:]), rb[:], ACT.Copy)
+            ra = keep.tile([P, W], F32, name=f"ra{m}")
+            nc.scalar.activation(ra[:], radicand[:], ACT.Sqrt)
+            nc.scalar.activation(res[:].indirect(n2_l[:]), ra[:], ACT.Copy)
+            nc.sync.dma_start(out[rows, :], res[:])

@@ -61,6 +61,9 @@ def tile_picked_hcodesendmxpolar_none_p_kernel(
         nc.vector.memset(plane1[:].bitcast(I32), 0)
         nc.vector.memset(plane2[:].bitcast(I32), 0)
 
+        warm = keep.tile([P, 1], F32, name="warm")
+        nc.scalar.activation(warm[:], gain[:, 0:1], ACT.Sqrt)
+
         def place_rows(plane, picked, queues):
             for j in range(4):
                 queues[j % len(queues)].dma_start(plane[j:P:32, :].bitcast(I32), picked[8 * j : P : 32, :].bitcast(I32))

@@ -49,12 +49,12 @@ def tile_picked_hcodesendmxpolar_none_p_kernel(
         nc.vector.memset(x_stab[:].bitcast(I32), 0)
         nc.scalar.dma_start(gain[:], gs.rearrange("(p t) o -> p (t o)", t=PACK))
         k1_l = load_list("k1_l", k1)
-        nc.scalar.dma_start(d_tab[:].bitcast(I32), d_words[0].rearrange("p n t -> p (n t)").bitcast(I32))
         offs_l = load_list("offs_l", offs)
-        nc.sync.dma_start(d_stab[0:P:8, :].bitcast(I32), d_scales[0].bitcast(I32))
-        nc.sync.dma_start(x_stab[0:P:8, :].bitcast(I32), x_scales[0].bitcast(I32))
         n1_l = load_list("n1_l", n1)
         k2_l = load_list("k2_l", k2)
+        nc.sync.dma_start(d_stab[0:P:8, :].bitcast(I32), d_scales[0].bitcast(I32))
+        nc.sync.dma_start(x_stab[0:P:8, :].bitcast(I32), x_scales[0].bitcast(I32))
+        nc.sync.dma_start(d_tab[:].bitcast(I32), d_words[0].rearrange("p n t -> p (n t)").bitcast(I32))
         nc.sync.dma_start(x_tab[:].bitcast(I32), x_words[0].rearrange("p n t -> p (n t)").bitcast(I32))
         n2_l = load_list("n2_l", n2)
         n3_l = load_list("n3_l", n3)
@@ -79,21 +79,20 @@ def tile_picked_hcodesendmxpolar_none_p_kernel(
         nc.vector.tensor_copy(xq[:], x_tab[:].indirect(offs_l[:]))
 
         w1_dealt = keep.tile([P, PACK, P], U32, name="w1_dealt", align_bytes=64)
+        nc.vector.tensor_copy(w1_dealt[:].rearrange("p t m -> p m t"), w1[:].rearrange("p (m t) -> p m t", t=PACK))
         s1_dealt = keep.tile([P, PACK, P], U8, name="s1_dealt", tag="bytes", align_bytes=64)
-        gh, ds = [], []
-        for t in range(PACK):
-            nc.vector.tensor_copy(w1_dealt[:, t, :], w1[:, t:H:PACK])
-            nc.vector.tensor_copy(s1_dealt[:, t, :], plane1[:, t:H:PACK])
-            gh.append(keep.tile([P, S], F32, name=f"gh{t}"))
-            ds.append(keep.tile([P, 2 * S], F32, name=f"ds{t}"))
-            for lo, hi in first_in_halves(t):
-                acc = psum.tile([P, S], F32, name="acc")
-                nc.tensor.matmul_mx(
-                    out=acc[:, lo:hi], lhsT=w1_dealt[:, t, :].bitcast(FP8X4), lhsT_scale=s1_dealt[:, t, :],
-                    rhs=xq[:, lo:hi].bitcast(FP8X4), rhs_scale=plane1[:, H + lo : H + hi], start=True, stop=True,
-                )
-                nc.vector.tensor_scalar(gh[t][:, lo:hi], acc[:, lo:hi], gain[:, t : t + 1], 0.0625, ALU.mult, ALU.mult)
-                nc.scalar.activation(ds[t][:].indirect(n1_l[:, lo // 16 : hi // 16]), gh[t][:, lo:hi], ACT.Copy)
+        gh = [keep.tile([P, S], F32, name=f"gh{t}") for t in range(PACK)]
+        ds = [keep.tile([P, 2 * S], F32, name=f"ds{t}") for t in range(PACK)]
+        for t, lo, hi in [(0, 0, HALF), (1, 0, S), (0, HALF, S), (2, 0, S), (3, 0, S)]:
+            if lo == 0:
+                nc.vector.tensor_copy(s1_dealt[:, t, :], plane1[:, t:H:PACK])
+            acc = psum.tile([P, S], F32, name="acc")
+            nc.tensor.matmul_mx(
+                out=acc[:, lo:hi], lhsT=w1_dealt[:, t, :].bitcast(FP8X4), lhsT_scale=s1_dealt[:, t, :],
+                rhs=xq[:, lo:hi].bitcast(FP8X4), rhs_scale=plane1[:, H + lo : H + hi], start=True, stop=True,
+            )
+            nc.vector.tensor_scalar(gh[t][:, lo:hi], acc[:, lo:hi], gain[:, t : t + 1], 0.0625, ALU.mult, ALU.mult)
+            nc.scalar.activation(ds[t][:].indirect(n1_l[:, lo // 16 : hi // 16]), gh[t][:, lo:hi], ACT.Copy)
 
         picked2 = keep.tile([P, H], U8, name="picked2", tag="bytes", align_bytes=64)
         nc.vector.tensor_copy(picked2[:], d_stab[:].indirect(k2_l[:]))
@@ -112,29 +111,42 @@ def tile_picked_hcodesendmxpolar_none_p_kernel(
             cols = slice(u * HALF, (u + 1) * HALF)
             nc.vector.quantize_mx(out=zq[:, cols].bitcast(FP8X4), scales=zs[:, cols], in_=z[u][:].rearrange("p c t -> p (c t)"))
 
-        for m in range(H // P):
+        def fetch_pairs(m):
             rows = slice(m * P, (m + 1) * P)
             h2 = keep.tile([P, S], F32, name=f"h2_{m}")
-            pieces = [slice(0, HALF), slice(HALF, S)] if m == 0 else [slice(0, S)]
-            for cols in pieces:
+            for lo, hi in first_in_halves(m):
                 acc = psum.tile([P, S], F32, name="acc")
                 nc.tensor.matmul_mx(
-                    out=acc[:, cols], lhsT=w2[:, rows].bitcast(FP8X4), lhsT_scale=plane2[:, rows],
-                    rhs=zq[:, cols].bitcast(FP8X4), rhs_scale=zs[:, cols], start=True, stop=True,
+                    out=acc[:, lo:hi], lhsT=w2[:, rows].bitcast(FP8X4), lhsT_scale=plane2[:, rows],
+                    rhs=zq[:, lo:hi].bitcast(FP8X4), rhs_scale=zs[:, lo:hi], start=True, stop=True,
                 )
-                nc.vector.tensor_scalar(h2[:, cols], acc[:, cols], 0.0625, None, ALU.mult)
+                nc.vector.tensor_scalar(h2[:, lo:hi], acc[:, lo:hi], 0.0625, None, ALU.mult)
             pab = keep.tile([P, 2, W], F32, name=f"pab{m}")
             nc.scalar.activation(pab[:, 0, :], h2[:].indirect(n2_l[:]), ACT.Copy)
             nc.scalar.activation(pab[:, 1, :], h2[:].indirect(n3_l[:]), ACT.Copy)
+            return pab
+
+        def make_rb(m, pab):
             rb = keep.tile([P, W], F32, name=f"rb{m}")
             nc.vector.scalar_tensor_tensor(rb[:], pab[:, 0, :], -0.5, pab[:, 1, :], ALU.mult, ALU.add)
+            return rb
+
+        def make_radicand(m, pab, radicand):
             sq = keep.tile([P, 2, W], F32, name=f"sq{m}")
             nc.vector.tensor_tensor(sq[:], pab[:], pab[:], ALU.mult)
-            radicand = keep.tile([P, W], F32, name=f"radicand{m}")
-            nc.vector.scalar_tensor_tensor(radicand[:], sq[:, 0, :], 0.25, sq[:, 1, :], ALU.add, ALU.add)
-            res = keep.tile([P, S], F32, name=f"res{m}")
-            nc.scalar.activation(res[:].indirect(n3_l[:]), rb[:], ACT.Copy)
-            ra = keep.tile([P, W], F32, name=f"ra{m}")
+            nc.vector.scalar_tensor_tensor(radicand, sq[:, 0, :], 0.25, sq[:, 1, :], ALU.add, ALU.add)
+
+        for first in range(0, H // P, 2):
+            second = first + 1
+            pab = [fetch_pairs(first), fetch_pairs(second)]
+            res = [keep.tile([P, S], F32, name=f"res{m}") for m in (first, second)]
+            radicand = keep.tile([P, 2, W], F32, name=f"radicand{first}")
+            ra = keep.tile([P, 2, W], F32, name=f"ra{first}")
+            nc.scalar.activation(res[0][:].indirect(n3_l[:]), make_rb(first, pab[0])[:], ACT.Copy)
+            make_radicand(first, pab[0], radicand[:, 0, :])
+            make_radicand(second, pab[1], radicand[:, 1, :])
             nc.scalar.activation(ra[:], radicand[:], ACT.Sqrt)
-            nc.scalar.activation(res[:].indirect(n2_l[:]), ra[:], ACT.Copy)
-            nc.sync.dma_start(out[rows, :], res[:])
+            nc.scalar.activation(res[1][:].indirect(n3_l[:]), make_rb(second, pab[1])[:], ACT.Copy)
+            for i in range(2):
+                nc.scalar.activation(res[i][:].indirect(n2_l[:]), ra[:, i, :], ACT.Copy)
+                nc.sync.dma_start(out[(first + i) * P : (first + i + 1) * P, :], res[i][:])

@@ -46,14 +46,14 @@ def tile_picked_hcodesendmxpolar_none_p_kernel(
         gain = keep.tile([P, PACK], F32, name="gain")
 
         nc.vector.memset(d_stab[:].bitcast(I32), 0)
-        nc.vector.memset(x_stab[:].bitcast(I32), 0)
+        nc.gpsimd.memset(x_stab[:].bitcast(I32), 0)
         nc.scalar.dma_start(gain[:], gs.rearrange("(p t) o -> p (t o)", t=PACK))
-        k1_l = load_list("k1_l", k1)
         offs_l = load_list("offs_l", offs)
+        k1_l = load_list("k1_l", k1)
+        nc.scalar.dma_start(x_stab[0:P:8, :].bitcast(I32), x_scales[0].bitcast(I32))
         n1_l = load_list("n1_l", n1)
         k2_l = load_list("k2_l", k2)
         nc.sync.dma_start(d_stab[0:P:8, :].bitcast(I32), d_scales[0].bitcast(I32))
-        nc.sync.dma_start(x_stab[0:P:8, :].bitcast(I32), x_scales[0].bitcast(I32))
         nc.sync.dma_start(d_tab[:].bitcast(I32), d_words[0].rearrange("p n t -> p (n t)").bitcast(I32))
         nc.sync.dma_start(x_tab[:].bitcast(I32), x_words[0].rearrange("p n t -> p (n t)").bitcast(I32))
         n2_l = load_list("n2_l", n2)
@@ -68,29 +68,34 @@ def tile_picked_hcodesendmxpolar_none_p_kernel(
             for j in range(4):
                 queues[j % len(queues)].dma_start(plane[j:P:32, :].bitcast(I32), picked[8 * j : P : 32, :].bitcast(I32))
 
-        picked1 = keep.tile([P, H + S], U8, name="picked1")
-        nc.vector.tensor_copy(picked1[:, 0:H], d_stab[:].indirect(k1_l[:]))
+        picked1 = keep.tile([P, H + S], U8, name="picked1", tag="picked", align_bytes=64)
         nc.vector.tensor_copy(picked1[:, H : H + S], x_stab[:].indirect(offs_l[:]))
+        nc.vector.tensor_copy(picked1[:, 0:H], d_stab[:].indirect(k1_l[:]))
         place_rows(plane1, picked1, [nc.sync, nc.scalar])
 
         w1 = keep.tile([P, H], U32, name="w1")
         nc.vector.tensor_copy(w1[:], d_tab[:].indirect(k1_l[:]))
-        xq = keep.tile([P, S], U32, name="xq", tag="words", align_bytes=64)
-        nc.vector.tensor_copy(xq[:], x_tab[:].indirect(offs_l[:]))
+        xq = [keep.tile([P, HALF], U32, name="xq0", tag="words", align_bytes=64)]
+        nc.vector.tensor_copy(xq[0][:], x_tab[:].indirect(offs_l[:, 0 : HALF // 16]))
 
         w1_dealt = keep.tile([P, PACK, P], U32, name="w1_dealt", align_bytes=64)
         nc.vector.tensor_copy(w1_dealt[:].rearrange("p t m -> p m t"), w1[:].rearrange("p (m t) -> p m t", t=PACK))
         s1_dealt = keep.tile([P, PACK, P], U8, name="s1_dealt", tag="bytes", align_bytes=64)
         gh = [keep.tile([P, S], F32, name=f"gh{t}") for t in range(PACK)]
         ds = [keep.tile([P, 2 * S], F32, name=f"ds{t}") for t in range(PACK)]
-        for t, lo, hi in [(0, 0, HALF), (1, 0, S), (0, HALF, S), (2, 0, S), (3, 0, S)]:
-            if lo == 0:
+        for t, halves in [(0, [0]), (1, [0, 1]), (0, [1]), (2, [0, 1]), (3, [0, 1])]:
+            if halves[0] == 0:
                 nc.vector.tensor_copy(s1_dealt[:, t, :], plane1[:, t:H:PACK])
+            if len(xq) < len(halves):
+                xq.append(keep.tile([P, HALF], U32, name="xq1", tag="picked", align_bytes=64))
+                nc.vector.tensor_copy(xq[1][:], x_tab[:].indirect(offs_l[:, HALF // 16 : S // 16]))
             acc = psum.tile([P, S], F32, name="acc")
-            nc.tensor.matmul_mx(
-                out=acc[:, lo:hi], lhsT=w1_dealt[:, t, :].bitcast(FP8X4), lhsT_scale=s1_dealt[:, t, :],
-                rhs=xq[:, lo:hi].bitcast(FP8X4), rhs_scale=plane1[:, H + lo : H + hi], start=True, stop=True,
-            )
+            for u in halves:
+                nc.tensor.matmul_mx(
+                    out=acc[:, u * HALF : (u + 1) * HALF], lhsT=w1_dealt[:, t, :].bitcast(FP8X4), lhsT_scale=s1_dealt[:, t, :],
+                    rhs=xq[u][:].bitcast(FP8X4), rhs_scale=plane1[:, H + u * HALF : H + (u + 1) * HALF], start=True, stop=True,
+                )
+            lo, hi = halves[0] * HALF, (halves[-1] + 1) * HALF
             nc.vector.tensor_scalar(gh[t][:, lo:hi], acc[:, lo:hi], gain[:, t : t + 1], 0.0625, ALU.mult, ALU.mult)
             nc.scalar.activation(ds[t][:].indirect(n1_l[:, lo // 16 : hi // 16]), gh[t][:, lo:hi], ACT.Copy)
 

@@ -30,6 +30,7 @@ def tile_picked_hcodesendmxpolar_none_p_kernel(
     with ExitStack() as ctx:
         lists = ctx.enter_context(tc.tile_pool(name="lists", bufs=1))
         keep = ctx.enter_context(tc.tile_pool(name="keep", bufs=1))
+        reuse = ctx.enter_context(tc.tile_pool(name="reuse", bufs=1))
         psum = ctx.enter_context(tc.psum_pool(name="psum", bufs=8))
 
         def load_list(name, src):
@@ -63,12 +64,14 @@ def tile_picked_hcodesendmxpolar_none_p_kernel(
 
         warm = keep.tile([P, 1], F32, name="warm")
         nc.scalar.activation(warm[:], gain[:, 0:1], ACT.Sqrt)
+        gain16 = keep.tile([P, PACK], F32, name="gain16")
+        nc.scalar.activation(gain16[:], gain[:], ACT.Copy, scale=0.0625)
 
         def place_rows(plane, picked, queues):
             for j in range(4):
                 queues[j % len(queues)].dma_start(plane[j:P:32, :].bitcast(I32), picked[8 * j : P : 32, :].bitcast(I32))
 
-        picked1 = keep.tile([P, H + S], U8, name="picked1", tag="picked", align_bytes=64)
+        picked1 = reuse.tile([P, H + S], U8, name="picked1", offset=0, align_bytes=64)
         nc.vector.tensor_copy(picked1[:, H : H + S], x_stab[:].indirect(offs_l[:]))
         nc.vector.tensor_copy(picked1[:, 0:H], d_stab[:].indirect(k1_l[:]))
         place_rows(plane1, picked1, [nc.sync, nc.scalar])
@@ -78,25 +81,30 @@ def tile_picked_hcodesendmxpolar_none_p_kernel(
         xq = [keep.tile([P, HALF], U32, name="xq0", tag="words", align_bytes=64)]
         nc.vector.tensor_copy(xq[0][:], x_tab[:].indirect(offs_l[:, 0 : HALF // 16]))
 
-        w1_dealt = keep.tile([P, PACK, P], U32, name="w1_dealt", align_bytes=64)
-        nc.vector.tensor_copy(w1_dealt[:].rearrange("p t m -> p m t"), w1[:].rearrange("p (m t) -> p m t", t=PACK))
+        w1_first = keep.tile([P, P], U32, name="w1_first", align_bytes=64)
+        w1_rest = reuse.tile([P, PACK - 1, P], U32, name="w1_rest", offset=4 * HALF, align_bytes=64)
+        w1_dealt = [w1_first[:]] + [w1_rest[:, t, :] for t in range(PACK - 1)]
         s1_dealt = keep.tile([P, PACK, P], U8, name="s1_dealt", tag="bytes", align_bytes=64)
         gh = [keep.tile([P, S], F32, name=f"gh{t}") for t in range(PACK)]
         ds = [keep.tile([P, 2 * S], F32, name=f"ds{t}") for t in range(PACK)]
-        for t, halves in [(0, [0]), (1, [0, 1]), (0, [1]), (2, [0, 1]), (3, [0, 1])]:
+        for t, halves in [(0, [0]), (1, [0]), (0, [1]), (1, [1]), (2, [0, 1]), (3, [0, 1])]:
             if halves[0] == 0:
+                nc.vector.tensor_copy(w1_dealt[t], w1[:, t:H:PACK])
                 nc.vector.tensor_copy(s1_dealt[:, t, :], plane1[:, t:H:PACK])
-            if len(xq) < len(halves):
-                xq.append(keep.tile([P, HALF], U32, name="xq1", tag="picked", align_bytes=64))
+            if len(xq) <= halves[-1]:
+                xq.append(reuse.tile([P, HALF], U32, name="xq1", offset=0, align_bytes=64))
                 nc.vector.tensor_copy(xq[1][:], x_tab[:].indirect(offs_l[:, HALF // 16 : S // 16]))
             acc = psum.tile([P, S], F32, name="acc")
             for u in halves:
                 nc.tensor.matmul_mx(
-                    out=acc[:, u * HALF : (u + 1) * HALF], lhsT=w1_dealt[:, t, :].bitcast(FP8X4), lhsT_scale=s1_dealt[:, t, :],
+                    out=acc[:, u * HALF : (u + 1) * HALF], lhsT=w1_dealt[t].bitcast(FP8X4), lhsT_scale=s1_dealt[:, t, :],
                     rhs=xq[u][:].bitcast(FP8X4), rhs_scale=plane1[:, H + u * HALF : H + (u + 1) * HALF], start=True, stop=True,
                 )
             lo, hi = halves[0] * HALF, (halves[-1] + 1) * HALF
-            nc.vector.tensor_scalar(gh[t][:, lo:hi], acc[:, lo:hi], gain[:, t : t + 1], 0.0625, ALU.mult, ALU.mult)
+            if (t, lo) == (0, 0):
+                nc.scalar.activation(gh[t][:, lo:hi], acc[:, lo:hi], ACT.Copy, scale=gain16[:, t : t + 1])
+            else:
+                nc.vector.tensor_scalar(gh[t][:, lo:hi], acc[:, lo:hi], gain16[:, t : t + 1], None, ALU.mult)
             nc.scalar.activation(ds[t][:].indirect(n1_l[:, lo // 16 : hi // 16]), gh[t][:, lo:hi], ACT.Copy)
 
         picked2 = keep.tile([P, H], U8, name="picked2", tag="bytes", align_bytes=64)

from contextlib import ExitStack

import concourse.mybir as mybir

F32 = mybir.dt.float32
BF16 = mybir.dt.bfloat16
I32 = mybir.dt.int32
U32 = mybir.dt.uint32
U16 = mybir.dt.uint16
U8 = mybir.dt.uint8
FP8X4 = mybir.dt.float8_e4m3fn_x4
ALU = mybir.AluOpType
ACT = mybir.ActivationFunctionType

P = 128
PACK = 4
T, S, G, H, W = 1024, 256, 2048, 512, 128
HALF = S // 2
FLOPS = 2 * 2 * 512 * H * S


def first_in_halves(tile_number):
    return [(0, HALF), (HALF, S)] if tile_number == 0 else [(0, S)]


def tile_picked_hcodesendmxpolar_none_p_kernel(
    tc, x_words, x_scales, d_words, d_scales, gs, offs, k1, n1, k2, n2, n3, out
):
    nc = tc.nc
    with ExitStack() as ctx:
        lists = ctx.enter_context(tc.tile_pool(name="lists", bufs=1))
        keep = ctx.enter_context(tc.tile_pool(name="keep", bufs=1))
        reuse = ctx.enter_context(tc.tile_pool(name="reuse", bufs=1))
        psum = ctx.enter_context(tc.psum_pool(name="psum", bufs=8))

        def load_list(name, src):
            t = lists.tile(list(src.shape), U16, name=name)
            nc.sync.dma_start(t[:], src)
            return t

        d_tab = keep.tile([P, G], U32, name="d_tab")
        x_tab = keep.tile([P, T], U32, name="x_tab")
        d_stab = keep.tile([P, G], U8, name="d_stab")
        x_stab = keep.tile([P, T], U8, name="x_stab")
        plane1 = keep.tile([P, H + S], U8, name="plane1", align_bytes=64)
        plane2 = keep.tile([P, H], U8, name="plane2", align_bytes=64)
        gain = keep.tile([P, PACK], F32, name="gain")

        nc.vector.memset(d_stab[:].bitcast(I32), 0)
        nc.gpsimd.memset(x_stab[:].bitcast(I32), 0)
        nc.scalar.dma_start(gain[:], gs.rearrange("(p t) o -> p (t o)", t=PACK))
        offs_l = load_list("offs_l", offs)
        k1_l = load_list("k1_l", k1)
        nc.scalar.dma_start(x_stab[0:P:8, :].bitcast(I32), x_scales[0].bitcast(I32))
        n1_l = load_list("n1_l", n1)
        k2_l = load_list("k2_l", k2)
        nc.sync.dma_start(d_stab[0:P:8, :].bitcast(I32), d_scales[0].bitcast(I32))
        nc.sync.dma_start(d_tab[:].bitcast(I32), d_words[0].rearrange("p n t -> p (n t)").bitcast(I32))
        nc.sync.dma_start(x_tab[:].bitcast(I32), x_words[0].rearrange("p n t -> p (n t)").bitcast(I32))
        n2_l = load_list("n2_l", n2)
        n3_l = load_list("n3_l", n3)
        nc.vector.memset(plane1[:].bitcast(I32), 0)
        nc.vector.memset(plane2[:].bitcast(I32), 0)

        warm = keep.tile([P, 1], F32, name="warm")
        nc.scalar.activation(warm[:], gain[:, 0:1], ACT.Sqrt)
        gain16 = keep.tile([P, PACK], F32, name="gain16")
        nc.scalar.activation(gain16[:], gain[:], ACT.Copy, scale=0.0625)

        def place_rows(plane, picked, queues):
            for j in range(4):
                queues[j % len(queues)].dma_start(plane[j:P:32, :].bitcast(I32), picked[8 * j : P : 32, :].bitcast(I32))

        picked1 = reuse.tile([P, H + S], U8, name="picked1", offset=0, align_bytes=64)
        nc.vector.tensor_copy(picked1[:, H : H + S], x_stab[:].indirect(offs_l[:]))
        nc.vector.tensor_copy(picked1[:, 0:H], d_stab[:].indirect(k1_l[:]))
        place_rows(plane1, picked1, [nc.sync, nc.scalar])

        w1 = keep.tile([P, H], U32, name="w1")
        nc.vector.tensor_copy(w1[:], d_tab[:].indirect(k1_l[:]))
        xq = [keep.tile([P, HALF], U32, name="xq0", tag="words", align_bytes=64)]
        nc.vector.tensor_copy(xq[0][:], x_tab[:].indirect(offs_l[:, 0 : HALF // 16]))

        w1_first = keep.tile([P, P], U32, name="w1_first", align_bytes=64)
        w1_rest = reuse.tile([P, PACK - 1, P], U32, name="w1_rest", offset=4 * HALF, align_bytes=64)
        w1_dealt = [w1_first[:]] + [w1_rest[:, t, :] for t in range(PACK - 1)]
        s1_dealt = keep.tile([P, PACK, P], U8, name="s1_dealt", tag="bytes", align_bytes=64)
        gh = [keep.tile([P, S], F32, name=f"gh{t}") for t in range(PACK)]
        ds = [keep.tile([P, 2 * S], F32, name=f"ds{t}") for t in range(PACK)]
        for t, halves in [(0, [0]), (1, [0]), (0, [1]), (1, [1]), (2, [0, 1]), (3, [0, 1])]:
            if halves[0] == 0:
                nc.vector.tensor_copy(w1_dealt[t], w1[:, t:H:PACK])
                nc.vector.tensor_copy(s1_dealt[:, t, :], plane1[:, t:H:PACK])
            if len(xq) <= halves[-1]:
                xq.append(reuse.tile([P, HALF], U32, name="xq1", offset=0, align_bytes=64))
                nc.vector.tensor_copy(xq[1][:], x_tab[:].indirect(offs_l[:, HALF // 16 : S // 16]))
            acc = psum.tile([P, S], F32, name="acc")
            for u in halves:
                nc.tensor.matmul_mx(
                    out=acc[:, u * HALF : (u + 1) * HALF], lhsT=w1_dealt[t].bitcast(FP8X4), lhsT_scale=s1_dealt[:, t, :],
                    rhs=xq[u][:].bitcast(FP8X4), rhs_scale=plane1[:, H + u * HALF : H + (u + 1) * HALF], start=True, stop=True,
                )
            lo, hi = halves[0] * HALF, (halves[-1] + 1) * HALF
            if (t, lo) == (0, 0):
                nc.scalar.activation(gh[t][:, lo:hi], acc[:, lo:hi], ACT.Copy, scale=gain16[:, t : t + 1])
            else:
                nc.vector.tensor_scalar(gh[t][:, lo:hi], acc[:, lo:hi], gain16[:, t : t + 1], None, ALU.mult)
            nc.scalar.activation(ds[t][:].indirect(n1_l[:, lo // 16 : hi // 16]), gh[t][:, lo:hi], ACT.Copy)

        picked2 = keep.tile([P, H], U8, name="picked2", tag="bytes", align_bytes=64)
        nc.vector.tensor_copy(picked2[:], d_stab[:].indirect(k2_l[:]))
        place_rows(plane2, picked2, [nc.sync])
        w2 = keep.tile([P, H], U32, name="w2", tag="words", align_bytes=64)
        nc.vector.tensor_copy(w2[:], d_tab[:].indirect(k2_l[:]))

        z = [keep.tile([P, HALF, PACK], BF16, name=f"z{u}", align_bytes=64) for u in range(2)]
        for t in range(PACK):
            for u in range(2):
                cols = slice(u * HALF, (u + 1) * HALF)
                nc.vector.tensor_tensor(z[u][:, :, t], gh[t][:, cols], ds[t][:, cols], ALU.subtract)
        zq = keep.tile([P, S], U32, name="zq", align_bytes=64)
        zs = keep.tile([P, S], U8, name="zs", align_bytes=64)
        for u in range(2):
            cols = slice(u * HALF, (u + 1) * HALF)
            nc.vector.quantize_mx(out=zq[:, cols].bitcast(FP8X4), scales=zs[:, cols], in_=z[u][:].rearrange("p c t -> p (c t)"))

        def fetch_pairs(m):
            rows = slice(m * P, (m + 1) * P)
            h2 = keep.tile([P, S], F32, name=f"h2_{m}")
            for lo, hi in first_in_halves(m):
                acc = psum.tile([P, S], F32, name="acc")
                nc.tensor.matmul_mx(
                    out=acc[:, lo:hi], lhsT=w2[:, rows].bitcast(FP8X4), lhsT_scale=plane2[:, rows],
                    rhs=zq[:, lo:hi].bitcast(FP8X4), rhs_scale=zs[:, lo:hi], start=True, stop=True,
                )
                nc.vector.tensor_scalar(h2[:, lo:hi], acc[:, lo:hi], 0.0625, None, ALU.mult)
            pab = keep.tile([P, 2, W], F32, name=f"pab{m}")
            nc.scalar.activation(pab[:, 0, :], h2[:].indirect(n2_l[:]), ACT.Copy)
            nc.scalar.activation(pab[:, 1, :], h2[:].indirect(n3_l[:]), ACT.Copy)
            return pab

        def make_rb(m, pab):
            rb = keep.tile([P, W], F32, name=f"rb{m}")
            nc.vector.scalar_tensor_tensor(rb[:], pab[:, 0, :], -0.5, pab[:, 1, :], ALU.mult, ALU.add)
            return rb

        def make_radicand(m, pab, radicand):
            sq = keep.tile([P, 2, W], F32, name=f"sq{m}")
            nc.vector.tensor_tensor(sq[:], pab[:], pab[:], ALU.mult)
            nc.vector.scalar_tensor_tensor(radicand, sq[:, 0, :], 0.25, sq[:, 1, :], ALU.add, ALU.add)

        for first in range(0, H // P, 2):
            second = first + 1
            pab = [fetch_pairs(first), fetch_pairs(second)]
            res = [keep.tile([P, S], F32, name=f"res{m}") for m in (first, second)]
            radicand = keep.tile([P, 2, W], F32, name=f"radicand{first}")
            ra = keep.tile([P, 2, W], F32, name=f"ra{first}")
            nc.scalar.activation(res[0][:].indirect(n3_l[:]), make_rb(first, pab[0])[:], ACT.Copy)
            make_radicand(first, pab[0], radicand[:, 0, :])
            make_radicand(second, pab[1], radicand[:, 1, :])
            nc.scalar.activation(ra[:], radicand[:], ACT.Sqrt)
            nc.scalar.activation(res[1][:].indirect(n3_l[:]), make_rb(second, pab[1])[:], ACT.Copy)
            for i in range(2):
                nc.scalar.activation(res[i][:].indirect(n2_l[:]), ra[:, i, :], ACT.Copy)
                nc.sync.dma_start(out[(first + i) * P : (first + i + 1) * P, :], res[i][:])
